import numpy as np
import ml_dtypes


def mxq(x, axis, fmt="e4m3"):
    dtype, down = {"e4m3": (ml_dtypes.float8_e4m3fn, 7), "e5m2": (ml_dtypes.float8_e5m2, 14)}[fmt]
    v = np.moveaxis(np.asarray(x, np.float32).astype(ml_dtypes.bfloat16).astype(np.float64), axis, -1)
    blocks = v.reshape(v.shape[:-1] + (-1, 32))
    amax = np.abs(blocks).max(-1, keepdims=True)
    byte = np.maximum(np.where(amax > 0, np.frexp(amax)[1] - 1 + 127, 0) - down, 1)
    scale = np.exp2(byte - 127.0)
    codes = (blocks / scale).astype(np.float32).astype(dtype).astype(np.float64)
    return np.moveaxis((codes * scale).reshape(v.shape), -1, axis)


WIDE = False


def mx_kscale(k):
    if not WIDE:
        return np.ones(k)
    levels = np.array([10, -10, 5, -5, 0])
    if k % 512:
        return np.exp2(np.random.permutation(np.resize(levels, k // 32))).repeat(32)
    a = np.empty((k // 512, 16))
    for p in range(k // 512):
        a[p, :8] = np.random.permutation(np.resize(levels, 8))
        for g in range(8):
            far = levels[np.abs(levels - a[p, g]) >= 10]
            a[p, g + 8] = far[np.random.randint(len(far))]
    return np.exp2(a.ravel()).repeat(32)


def f64(x):
    return np.asarray(x).astype(np.float64)


def striped(idx):
    return np.tile(idx.reshape(-1, 16).T, (8, 1)).astype(np.uint16)


def unstriped(offs):
    return offs[:16].T.reshape(-1).astype(np.int64)


def pack_weight(w):
    k, n = w.shape
    w = f64(np.asarray(w, np.float32).astype(ml_dtypes.bfloat16)).reshape(k // 32, 32, n)
    amax = np.abs(w).max(1)
    byte = np.clip(np.where(amax > 0, np.frexp(amax)[1] - 1 + 127 - 7, 1), 1, 254)
    scaled = (w * np.exp2(127.0 - byte)[:, None, :]).reshape(k, n).astype(np.float32)
    words = np.ascontiguousarray(scaled.reshape(k // 512, 128, 4, n).transpose(0, 1, 3, 2)).astype(ml_dtypes.float8_e4m3fn).view(np.uint8)
    return words, np.ascontiguousarray(byte.astype(np.uint8).reshape(k // 512, 16, n))


def unpack_weight(words, scales):
    g, p, n, _ = words.shape
    vals = np.ascontiguousarray(words).view(ml_dtypes.float8_e4m3fn).astype(np.float64) * np.repeat(np.exp2(scales.astype(np.float64) - 127.0), 8, axis=1)[..., None]
    return vals.transpose(0, 1, 3, 2).reshape(g * 512, n)


def sigmoid(v):
    return 1.0 / (1.0 + np.exp(-np.maximum(v, -700.0)))


K, T, S, N = 512, 2048, 512, 256


def setup_inputs():
    n = np.random.standard_normal
    s = mx_kscale(K)[:, None]
    packed_xT = pack_weight(n((K, T)) * s)
    return {
        "x_words": packed_xT[0],
        "x_scales": packed_xT[1],
        "w0": (n((K, N)) / np.sqrt(3 * K) / s).astype(np.float32),
        "v0": (n((K, N)) / np.sqrt(3 * K) / s).astype(np.float32),
        "w1": (n((K, N)) / np.sqrt(3 * K) / s).astype(np.float32),
        "v1": (n((K, N)) / np.sqrt(3 * K) / s).astype(np.float32),
        "w2": (n((K, N)) / np.sqrt(3 * K) / s).astype(np.float32),
        "v2": (n((K, N)) / np.sqrt(3 * K) / s).astype(np.float32),
        "offs": striped(np.random.permutation(T)[:S]),
        "back1": striped(np.random.permutation(T)[:S]),
        "back2": striped(np.random.permutation(T)[:S]),
    }


def reference(x_words, x_scales, w0, v0, w1, v1, w2, v2, offs, back1, back2):
    xq = unpack_weight(x_words, x_scales)[:, unstriped(offs)]
    x_back1 = unpack_weight(x_words, x_scales)[:, unstriped(back1)]
    x_back2 = unpack_weight(x_words, x_scales)[:, unstriped(back2)]
    f = np.tanh(mxq(f64(w0), 0, "e4m3").T @ xq + mxq(f64(w1), 0, "e4m3").T @ x_back1 + mxq(f64(w2), 0, "e4m3").T @ x_back2)
    g = sigmoid(mxq(f64(v0), 0, "e4m3").T @ xq + mxq(f64(v1), 0, "e4m3").T @ x_back1 + mxq(f64(v2), 0, "e4m3").T @ x_back2)
    return f * g

@@ -1,0 +1,132 @@
+from contextlib import ExitStack
+
+import concourse.mybir as mybir
+
+K, T, S, N = 512, 2048, 512, 256
+FLOPS = 2 * 6 * K * N * S
+
+F32 = mybir.dt.float32
+BF16 = mybir.dt.bfloat16
+I32 = mybir.dt.int32
+U32 = mybir.dt.uint32
+U16 = mybir.dt.uint16
+U8 = mybir.dt.uint8
+FP8X4 = mybir.dt.float8_e4m3fn_x4
+ACT = mybir.ActivationFunctionType
+MULT = mybir.AluOpType.mult
+
+P = 128
+PACK = 4
+HALF = S // 2
+M = 128
+
+
+def tile_picked_zwave_tanh_p_kernel(tc, x_words, x_scales, w0, v0, w1, v1, w2, v2, offs, back1, back2, out):
+    nc = tc.nc
+    with ExitStack() as ctx:
+        keep = ctx.enter_context(tc.tile_pool(name="keep", bufs=1))
+        psum = ctx.enter_context(tc.psum_pool(name="psum", bufs=1))
+
+        lists = [keep.tile([P, S // 16], U16, name="list%d" % d) for d in range(3)]
+        table_words = keep.tile([P, T], U32, name="table_words", align_bytes=64)
+        table_scales = keep.tile([P, T], U8, name="table_scales", align_bytes=64)
+
+        def load(weight, name, cols):
+            width = cols.stop - cols.start
+            raw = keep.tile([P, PACK, width], F32, name=name + "_raw", tag=name + "_raw", align_bytes=64)
+            nc.sync.dma_start(out=raw[:], in_=weight.rearrange("(p t) n -> p t n", t=PACK)[:, :, cols])
+            return raw
+
+        def cast(raw, name, on_vector):
+            width = raw.shape[2]
+            grouped = keep.tile([P, width, PACK], BF16, name=name + "_bf16", align_bytes=64)
+            dst = grouped[:].rearrange("p (c i) t -> p c t i", i=4)
+            src = raw[:].rearrange("p t (c i) -> p c t i", i=4)
+            if on_vector:
+                nc.vector.tensor_copy(out=dst, in_=src)
+            else:
+                nc.scalar.copy(out=dst, in_=src)
+            return grouped
+
+        def quantize(grouped, name):
+            width = grouped.shape[1]
+            codes = keep.tile([P, width], U32, name=name + "_codes", align_bytes=64)
+            scales = keep.tile([P, width], U8, name=name + "_scales", align_bytes=64)
+            nc.vector.quantize_mx(out=codes[:].bitcast(FP8X4), scales=scales[:], in_=grouped[:].rearrange("p n t -> p (n t)"))
+            return [(codes[:, c : c + M], scales[:, c : c + M]) for c in range(0, width, M)]
+
+        nc.vector.memset(table_scales[:].bitcast(I32), 0)
+        nc.sync.dma_start(lists[0][:], offs)
+        whole = slice(0, N)
+        raw = {}
+        raw["v0"] = load(v0, "v0", whole)
+        for r in range(4):
+            nc.scalar.dma_start(out=table_scales[r:P:32, :].bitcast(I32), in_=x_scales[0, r:16:4, :].bitcast(I32))
+        raw["v1"] = load(v1, "v1", whole)
+        nc.sync.dma_start(lists[1][:], back1)
+        nc.sync.dma_start(lists[2][:], back2)
+        raw["v2"] = load(v2, "v2", whole)
+        nc.sync.dma_start(out=table_words[:].bitcast(I32), in_=x_words[0].rearrange("p n t -> p (n t)").bitcast(I32))
+        raw["w0"] = load(w0, "w0", whole)
+        raw["w1"] = load(w1, "w1", whole)
+        raw["w2a"] = load(w2, "w2a", slice(0, M))
+        raw["w2b"] = load(w2, "w2b", slice(M, N))
+
+        picked_scales = []
+        for d in range(3):
+            ps = keep.tile([P, S], U8, name="picked_scales%d" % d, align_bytes=64)
+            nc.vector.tensor_copy(ps[:], table_scales[:].indirect(lists[d][:]))
+            picked_scales.append(ps)
+
+        wq = [quantize(cast(raw[name], name, False), name) for name in ("v0", "v1", "v2")]
+
+        picked_words = {}
+        for h in range(2):
+            for d in range(3):
+                pw = keep.tile([P, HALF], U32, name="picked_words%d_%d" % (d, h), align_bytes=64)
+                nc.vector.tensor_copy(pw[:], table_words[:].indirect(lists[d][:, h * HALF // 16 : (h + 1) * HALF // 16]))
+                picked_words[d, h] = pw
+
+        def product(bank, quantized, d, m, h):
+            codes, scales = quantized[m]
+            nc.tensor.matmul_mx(
+                out=bank[:, 0:HALF],
+                lhsT=codes.bitcast(FP8X4),
+                lhsT_scale=scales,
+                rhs=picked_words[d, h][:].bitcast(FP8X4),
+                rhs_scale=picked_scales[d][:, h * HALF : (h + 1) * HALF],
+                start=(d == 0),
+                stop=(d == 2),
+            )
+
+        f_bank = {(m, h): psum.tile([P, 512], F32, name="f_bank%d_%d" % (m, h)) for h in range(2) for m in range(2)}
+        g_bank = {(m, h): psum.tile([P, 512], F32, name="g_bank%d_%d" % (m, h)) for h in range(2) for m in range(2)}
+        for h in range(2):
+            for d in range(3):
+                for m in range(2):
+                    product(f_bank[m, h], wq[d], d, m, h)
+
+        f = {}
+        vq = []
+        for h, name in enumerate(("w0", "w1")):
+            vq.append(quantize(cast(raw[name], name, False), name))
+            fh = keep.tile([P, 2, HALF], F32, name="f%d" % h, tag=name + "_raw", align_bytes=64)
+            for m in range(2):
+                nc.scalar.activation(out=fh[:, m, :], in_=f_bank[m, h][:, 0:HALF], func=ACT.Sigmoid)
+                f[m, h] = fh[:, m, :]
+        ga = cast(raw["w2a"], "w2a", True)
+        gb = cast(raw["w2b"], "w2b", True)
+        vq.append(quantize(ga, "w2a") + quantize(gb, "w2b"))
+
+        for d in range(2):
+            for h in range(2):
+                for m in range(2):
+                    product(g_bank[m, h], vq[d], d, m, h)
+        for m in range(2):
+            for h in range(2):
+                product(g_bank[m, h], vq[2], 2, m, h)
+                g = keep.tile([P, HALF], F32, name="g%d_%d" % (m, h))
+                nc.scalar.activation(out=g[:], in_=g_bank[m, h][:, 0:HALF], func=ACT.Tanh)
+                y = keep.tile([P, HALF], F32, name="y%d_%d" % (m, h))
+                nc.vector.tensor_tensor(out=y[:], in0=f[m, h], in1=g[:], op=MULT)
+                nc.sync.dma_start(out=out[m * M : (m + 1) * M, h * HALF : (h + 1) * HALF], in_=y[:])

@@ -31,17 +31,17 @@ def tile_picked_zwave_tanh_p_kernel(tc, x_words, x_scales, w0, v0, w1, v1, w2, v
         table_words = keep.tile([P, T], U32, name="table_words", align_bytes=64)
         table_scales = keep.tile([P, T], U8, name="table_scales", align_bytes=64)
 
-        def load(weight, name, cols):
+        def load(weight, name, cols=slice(0, N)):
             width = cols.stop - cols.start
             raw = keep.tile([P, PACK, width], F32, name=name + "_raw", tag=name + "_raw", align_bytes=64)
             nc.sync.dma_start(out=raw[:], in_=weight.rearrange("(p t) n -> p t n", t=PACK)[:, :, cols])
             return raw
 
-        def cast(raw, name, on_vector):
-            width = raw.shape[2]
-            grouped = keep.tile([P, width, PACK], BF16, name=name + "_bf16", align_bytes=64)
+        def cast(name, on_vector=False):
+            width = raw[name].shape[2]
+            grouped = keep.tile([P, width, PACK], BF16, name=name + "_bf16", tag=name + "_bf16", align_bytes=64)
             dst = grouped[:].rearrange("p (c i) t -> p c t i", i=4)
-            src = raw[:].rearrange("p t (c i) -> p c t i", i=4)
+            src = raw[name][:].rearrange("p t (c i) -> p c t i", i=4)
             if on_vector:
                 nc.vector.tensor_copy(out=dst, in_=src)
             else:
@@ -55,20 +55,32 @@ def tile_picked_zwave_tanh_p_kernel(tc, x_words, x_scales, w0, v0, w1, v1, w2, v
             nc.vector.quantize_mx(out=codes[:].bitcast(FP8X4), scales=scales[:], in_=grouped[:].rearrange("p n t -> p (n t)"))
             return [(codes[:, c : c + M], scales[:, c : c + M]) for c in range(0, width, M)]
 
+        def load_list(d):
+            nc.sync.dma_start(lists[d][:], (offs, back1, back2)[d])
+
+        def load_scales(queue):
+            for r in range(4):
+                queue.dma_start(out=table_scales[r:P:32, :].bitcast(I32), in_=x_scales[0, r:16:4, :].bitcast(I32))
+
+        def load_words():
+            nc.sync.dma_start(out=table_words[:].bitcast(I32), in_=x_words[0].rearrange("p n t -> p (n t)").bitcast(I32))
+
         nc.vector.memset(table_scales[:].bitcast(I32), 0)
-        nc.sync.dma_start(lists[0][:], offs)
-        whole = slice(0, N)
+        warm_in = keep.tile([P, 1], F32, name="warm_in")
+        warm_out = keep.tile([P, 1], F32, name="warm_out")
+        nc.gpsimd.memset(warm_in[:], 0.0)
         raw = {}
-        raw["v0"] = load(v0, "v0", whole)
-        for r in range(4):
-            nc.scalar.dma_start(out=table_scales[r:P:32, :].bitcast(I32), in_=x_scales[0, r:16:4, :].bitcast(I32))
-        raw["v1"] = load(v1, "v1", whole)
-        nc.sync.dma_start(lists[1][:], back1)
-        nc.sync.dma_start(lists[2][:], back2)
-        raw["v2"] = load(v2, "v2", whole)
-        nc.sync.dma_start(out=table_words[:].bitcast(I32), in_=x_words[0].rearrange("p n t -> p (n t)").bitcast(I32))
-        raw["w0"] = load(w0, "w0", whole)
-        raw["w1"] = load(w1, "w1", whole)
+        nc.scalar.activation(out=warm_out[:], in_=warm_in[:], func=ACT.Sigmoid)
+        load_list(0)
+        load_list(1)
+        load_scales(nc.sync)
+        raw["v0"] = load(v0, "v0")
+        load_list(2)
+        load_words()
+        raw["w0"] = load(w0, "w0")
+        raw["v1"] = load(v1, "v1")
+        raw["v2"] = load(v2, "v2")
+        raw["w1"] = load(w1, "w1")
         raw["w2a"] = load(w2, "w2a", slice(0, M))
         raw["w2b"] = load(w2, "w2b", slice(M, N))
 
@@ -78,55 +90,66 @@ def tile_picked_zwave_tanh_p_kernel(tc, x_words, x_scales, w0, v0, w1, v1, w2, v
             nc.vector.tensor_copy(ps[:], table_scales[:].indirect(lists[d][:]))
             picked_scales.append(ps)
 
-        wq = [quantize(cast(raw[name], name, False), name) for name in ("v0", "v1", "v2")]
-
         picked_words = {}
-        for h in range(2):
-            for d in range(3):
-                pw = keep.tile([P, HALF], U32, name="picked_words%d_%d" % (d, h), align_bytes=64)
-                nc.vector.tensor_copy(pw[:], table_words[:].indirect(lists[d][:, h * HALF // 16 : (h + 1) * HALF // 16]))
-                picked_words[d, h] = pw
 
-        def product(bank, quantized, d, m, h):
-            codes, scales = quantized[m]
+        def gather_words(d, tag):
+            pw = keep.tile([P, S], U32, name="picked_words%d" % d, tag=tag, align_bytes=64)
+            nc.vector.tensor_copy(pw[:], table_words[:].indirect(lists[d][:]))
+            picked_words[d] = pw
+
+        def product(bank, quantized, d, cols):
+            codes, scales = quantized
             nc.tensor.matmul_mx(
-                out=bank[:, 0:HALF],
+                out=bank[:, 0 : cols.stop - cols.start],
                 lhsT=codes.bitcast(FP8X4),
                 lhsT_scale=scales,
-                rhs=picked_words[d, h][:].bitcast(FP8X4),
-                rhs_scale=picked_scales[d][:, h * HALF : (h + 1) * HALF],
+                rhs=picked_words[d][:, cols].bitcast(FP8X4),
+                rhs_scale=picked_scales[d][:, cols],
                 start=(d == 0),
                 stop=(d == 2),
             )
 
-        f_bank = {(m, h): psum.tile([P, 512], F32, name="f_bank%d_%d" % (m, h)) for h in range(2) for m in range(2)}
-        g_bank = {(m, h): psum.tile([P, 512], F32, name="g_bank%d_%d" % (m, h)) for h in range(2) for m in range(2)}
-        for h in range(2):
-            for d in range(3):
-                for m in range(2):
-                    product(f_bank[m, h], wq[d], d, m, h)
+        halves = [slice(h * HALF, (h + 1) * HALF) for h in range(2)]
+        f_bank = {(m, h): psum.tile([P, 512], F32, name="f_bank%d_%d" % (m, h)) for m in range(2) for h in range(2)}
+        g_bank = [psum.tile([P, 512], F32, name="g_bank%d" % m) for m in range(2)]
 
-        f = {}
-        vq = []
-        for h, name in enumerate(("w0", "w1")):
-            vq.append(quantize(cast(raw[name], name, False), name))
-            fh = keep.tile([P, 2, HALF], F32, name="f%d" % h, tag=name + "_raw", align_bytes=64)
+        def g_products(quantized, d):
             for m in range(2):
-                nc.scalar.activation(out=fh[:, m, :], in_=f_bank[m, h][:, 0:HALF], func=ACT.Sigmoid)
-                f[m, h] = fh[:, m, :]
-        ga = cast(raw["w2a"], "w2a", True)
-        gb = cast(raw["w2b"], "w2b", True)
-        vq.append(quantize(ga, "w2a") + quantize(gb, "w2b"))
+                product(g_bank[m], quantized[m], d, slice(0, S))
 
-        for d in range(2):
+        def f_products(quantized, d, ms=(0, 1)):
+            for i, m in enumerate(ms):
+                for h in range(2):
+                    product(f_bank[m, h], quantized[i], d, halves[h])
+
+        def sigmoids(tag):
+            g = keep.tile([P, 2, S], F32, name="g", tag=tag, align_bytes=64)
+            for m in range(2):
+                nc.scalar.activation(out=g[:, m, :], in_=g_bank[m][:], func=ACT.Sigmoid)
+            return g
+
+        def finish(m):
             for h in range(2):
-                for m in range(2):
-                    product(g_bank[m, h], vq[d], d, m, h)
-        for m in range(2):
-            for h in range(2):
-                product(g_bank[m, h], vq[2], 2, m, h)
-                g = keep.tile([P, HALF], F32, name="g%d_%d" % (m, h))
-                nc.scalar.activation(out=g[:], in_=g_bank[m, h][:, 0:HALF], func=ACT.Tanh)
+                f = keep.tile([P, HALF], F32, name="f%d_%d" % (m, h))
+                nc.scalar.activation(out=f[:], in_=f_bank[m, h][:, 0:HALF], func=ACT.Tanh)
                 y = keep.tile([P, HALF], F32, name="y%d_%d" % (m, h))
-                nc.vector.tensor_tensor(out=y[:], in0=f[m, h], in1=g[:], op=MULT)
-                nc.sync.dma_start(out=out[m * M : (m + 1) * M, h * HALF : (h + 1) * HALF], in_=y[:])
+                nc.vector.tensor_tensor(out=y[:], in0=f[:], in1=g[:, m, halves[h]], op=MULT)
+                nc.sync.dma_start(out=out[m * M : (m + 1) * M, halves[h]], in_=y[:])
+
+        qv0 = quantize(cast("v0"), "v0")
+        gather_words(0, "pw0")
+        g_products(qv0, 0)
+        gather_words(1, "pw1")
+        qw0 = quantize(cast("w0"), "w0")
+        f_products(qw0, 0)
+        gather_words(2, "w0_bf16")
+        g_products(quantize(cast("v1"), "v1"), 1)
+        g_products(quantize(cast("v2"), "v2"), 2)
+        bw1 = cast("w1")
+        ba = cast("w2a", True)
+        f_products(quantize(bw1, "w1"), 1)
+        g = sigmoids("w1_raw")
+        f_products(quantize(ba, "w2a"), 2, (0,))
+        f_products(quantize(cast("w2b", True), "w2b"), 2, (1,))
+        finish(0)
+        finish(1)

@@ -53,6 +53,7 @@ def tile_picked_zwave_tanh_p_kernel(tc, x_words, x_scales, w0, v0, w1, v1, w2, v
             codes = keep.tile([P, width], U32, name=name + "_codes", align_bytes=64)
             scales = keep.tile([P, width], U8, name=name + "_scales", align_bytes=64)
             nc.vector.quantize_mx(out=codes[:].bitcast(FP8X4), scales=scales[:], in_=grouped[:].rearrange("p n t -> p (n t)"))
+            whole[name] = (codes, scales)
             return [(codes[:, c : c + M], scales[:, c : c + M]) for c in range(0, width, M)]
 
         def load_list(d):
@@ -70,6 +71,7 @@ def tile_picked_zwave_tanh_p_kernel(tc, x_words, x_scales, w0, v0, w1, v1, w2, v
         warm_out = keep.tile([P, 1], F32, name="warm_out")
         nc.gpsimd.memset(warm_in[:], 0.0)
         raw = {}
+        whole = {}
         nc.scalar.activation(out=warm_out[:], in_=warm_in[:], func=ACT.Sigmoid)
         load_list(0)
         load_list(1)
@@ -77,9 +79,9 @@ def tile_picked_zwave_tanh_p_kernel(tc, x_words, x_scales, w0, v0, w1, v1, w2, v
         raw["v0"] = load(v0, "v0")
         load_list(2)
         load_words()
-        raw["w0"] = load(w0, "w0")
         raw["v1"] = load(v1, "v1")
         raw["v2"] = load(v2, "v2")
+        raw["w0"] = load(w0, "w0")
         raw["w1"] = load(w1, "w1")
         raw["w2a"] = load(w2, "w2a", slice(0, M))
         raw["w2b"] = load(w2, "w2b", slice(M, N))
@@ -109,18 +111,31 @@ def tile_picked_zwave_tanh_p_kernel(tc, x_words, x_scales, w0, v0, w1, v1, w2, v
                 stop=(d == 2),
             )
 
-        halves = [slice(h * HALF, (h + 1) * HALF) for h in range(2)]
-        f_bank = {(m, h): psum.tile([P, 512], F32, name="f_bank%d_%d" % (m, h)) for m in range(2) for h in range(2)}
+        pieces = [[(0, 256), (256, 512)], [(0, 256), (256, 384), (384, 512)]]
+        f_bank = {(m, c): psum.tile([P, 512], F32, name="f_bank%d_%d" % (m, c)) for m in range(2) for c, e in pieces[m]}
         g_bank = [psum.tile([P, 512], F32, name="g_bank%d" % m) for m in range(2)]
 
         def g_products(quantized, d):
             for m in range(2):
                 product(g_bank[m], quantized[m], d, slice(0, S))
 
-        def f_products(quantized, d, ms=(0, 1)):
-            for i, m in enumerate(ms):
-                for h in range(2):
-                    product(f_bank[m, h], quantized[i], d, halves[h])
+        def f_products(quantized, d, m):
+            for c, e in pieces[m]:
+                product(f_bank[m, c], quantized, d, slice(c, e))
+
+        def warm_tensor(name, passes):
+            codes, scales = whole[name]
+            spare = psum.tile([P, 512], F32, name="spare_bank")
+            for i in range(passes):
+                nc.tensor.matmul_mx(
+                    out=spare[:, 0:N],
+                    lhsT=codes[:, 0:M].bitcast(FP8X4),
+                    lhsT_scale=scales[:, 0:M],
+                    rhs=codes[:].bitcast(FP8X4),
+                    rhs_scale=scales[:],
+                    start=True,
+                    stop=True,
+                )
 
         def sigmoids(tag):
             g = keep.tile([P, 2, S], F32, name="g", tag=tag, align_bytes=64)
@@ -129,27 +144,30 @@ def tile_picked_zwave_tanh_p_kernel(tc, x_words, x_scales, w0, v0, w1, v1, w2, v
             return g
 
         def finish(m):
-            for h in range(2):
-                f = keep.tile([P, HALF], F32, name="f%d_%d" % (m, h))
-                nc.scalar.activation(out=f[:], in_=f_bank[m, h][:, 0:HALF], func=ACT.Tanh)
-                y = keep.tile([P, HALF], F32, name="y%d_%d" % (m, h))
-                nc.vector.tensor_tensor(out=y[:], in0=f[:], in1=g[:, m, halves[h]], op=MULT)
-                nc.sync.dma_start(out=out[m * M : (m + 1) * M, halves[h]], in_=y[:])
+            for c, e in pieces[m]:
+                f = keep.tile([P, e - c], F32, name="f%d_%d" % (m, c))
+                nc.scalar.activation(out=f[:], in_=f_bank[m, c][:, 0 : e - c], func=ACT.Tanh)
+                y = keep.tile([P, e - c], F32, name="y%d_%d" % (m, c))
+                nc.vector.tensor_tensor(out=y[:], in0=f[:], in1=g[:, m, c:e], op=MULT)
+                nc.sync.dma_start(out=out[m * M : (m + 1) * M, c:e], in_=y[:])
 
         qv0 = quantize(cast("v0"), "v0")
         gather_words(0, "pw0")
         g_products(qv0, 0)
         gather_words(1, "pw1")
-        qw0 = quantize(cast("w0"), "w0")
-        f_products(qw0, 0)
-        gather_words(2, "w0_bf16")
         g_products(quantize(cast("v1"), "v1"), 1)
+        gather_words(2, "v1_bf16")
         g_products(quantize(cast("v2"), "v2"), 2)
+        qw0 = quantize(cast("w0"), "w0")
+        f_products(qw0[0], 0, 0)
+        f_products(qw0[1], 0, 1)
         bw1 = cast("w1")
         ba = cast("w2a", True)
-        f_products(quantize(bw1, "w1"), 1)
+        qw1 = quantize(bw1, "w1")
+        f_products(qw1[0], 1, 0)
         g = sigmoids("w1_raw")
-        f_products(quantize(ba, "w2a"), 2, (0,))
-        f_products(quantize(cast("w2b", True), "w2b"), 2, (1,))
+        f_products(quantize(ba, "w2a")[0], 2, 0)
+        f_products(qw1[1], 1, 1)
+        f_products(quantize(cast("w2b", True), "w2b")[0], 2, 1)
         finish(0)
         finish(1)

@@ -48,19 +48,20 @@ def tile_picked_zwave_tanh_p_kernel(tc, x_words, x_scales, w0, v0, w1, v1, w2, v
                 nc.scalar.copy(out=dst, in_=src)
             return grouped
 
-        def quantize(grouped, name):
-            width = grouped.shape[1]
-            codes = keep.tile([P, width], U32, name=name + "_codes", align_bytes=64)
+        def quantize(grouped, name, cols=None, tag=None):
+            cols = cols or slice(0, grouped.shape[1])
+            width = cols.stop - cols.start
+            codes = keep.tile([P, width], U32, name=name + "_codes", tag=tag or name + "_codes", align_bytes=64)
             scales = keep.tile([P, width], U8, name=name + "_scales", align_bytes=64)
-            nc.vector.quantize_mx(out=codes[:].bitcast(FP8X4), scales=scales[:], in_=grouped[:].rearrange("p n t -> p (n t)"))
+            nc.vector.quantize_mx(out=codes[:].bitcast(FP8X4), scales=scales[:], in_=grouped[:, cols, :].rearrange("p n t -> p (n t)"))
             whole[name] = (codes, scales)
             return [(codes[:, c : c + M], scales[:, c : c + M]) for c in range(0, width, M)]
 
         def load_list(d):
             nc.sync.dma_start(lists[d][:], (offs, back1, back2)[d])
 
-        def load_scales(queue):
-            for r in range(4):
+        def load_scales(queue, rows):
+            for r in rows:
                 queue.dma_start(out=table_scales[r:P:32, :].bitcast(I32), in_=x_scales[0, r:16:4, :].bitcast(I32))
 
         def load_words():
@@ -69,13 +70,14 @@ def tile_picked_zwave_tanh_p_kernel(tc, x_words, x_scales, w0, v0, w1, v1, w2, v
         nc.vector.memset(table_scales[:].bitcast(I32), 0)
         warm_in = keep.tile([P, 1], F32, name="warm_in")
         warm_out = keep.tile([P, 1], F32, name="warm_out")
-        nc.gpsimd.memset(warm_in[:], 0.0)
+        nc.vector.memset(warm_in[:], 0.0)
         raw = {}
         whole = {}
-        nc.scalar.activation(out=warm_out[:], in_=warm_in[:], func=ACT.Sigmoid)
         load_list(0)
         load_list(1)
-        load_scales(nc.sync)
+        load_scales(nc.scalar, (2, 3))
+        load_scales(nc.sync, (0, 1))
+        nc.scalar.activation(out=warm_out[:], in_=warm_in[:], func=ACT.Sigmoid)
         raw["v0"] = load(v0, "v0")
         load_list(2)
         load_words()

@@ -3,7 +3,8 @@ from contextlib import ExitStack
 import concourse.mybir as mybir
 
 K, T, S, N = 512, 2048, 512, 256
-FLOPS = 2 * 6 * K * N * S
+TAPS = 3
+FLOPS = 2 * (2 * TAPS) * K * N * S
 
 F32 = mybir.dt.float32
 BF16 = mybir.dt.bfloat16
@@ -17,8 +18,15 @@ MULT = mybir.AluOpType.mult
 
 P = 128
 PACK = 4
-HALF = S // 2
+QUADRANT = 32
+SCALE_ROWS = K // 32
+LIST_GROUP = 16
+RUN = 4
 M = 128
+BANK = 512
+HALF = S // 2
+ALIGN = 64
+SCALAR_SHARE = 64
 
 
 def tile_picked_zwave_tanh_p_kernel(tc, x_words, x_scales, w0, v0, w1, v1, w2, v2, offs, back1, back2, out):
@@ -27,82 +35,71 @@ def tile_picked_zwave_tanh_p_kernel(tc, x_words, x_scales, w0, v0, w1, v1, w2, v
         keep = ctx.enter_context(tc.tile_pool(name="keep", bufs=1))
         psum = ctx.enter_context(tc.psum_pool(name="psum", bufs=1))
 
-        lists = [keep.tile([P, S // 16], U16, name="list%d" % d) for d in range(3)]
-        table_words = keep.tile([P, T], U32, name="table_words", align_bytes=64)
-        table_scales = keep.tile([P, T], U8, name="table_scales", align_bytes=64)
+        lists = [keep.tile([P, S // LIST_GROUP], U16, name="list%d" % d) for d in range(TAPS)]
+        table_words = keep.tile([P, T], U32, name="table_words", align_bytes=ALIGN)
+        table_scales = keep.tile([P, T], U8, name="table_scales", align_bytes=ALIGN)
 
-        def load(weight, name, cols=slice(0, N)):
-            width = cols.stop - cols.start
-            raw = keep.tile([P, PACK, width], F32, name=name + "_raw", tag=name + "_raw", align_bytes=64)
+        def load(weight, name, cols):
+            raw = keep.tile([P, PACK, cols.stop - cols.start], F32, name=name, tag=name, align_bytes=ALIGN)
             nc.sync.dma_start(out=raw[:], in_=weight.rearrange("(p t) n -> p t n", t=PACK)[:, :, cols])
             return raw
 
-        def cast(name, on_vector=False):
-            width = raw[name].shape[2]
-            grouped = keep.tile([P, width, PACK], BF16, name=name + "_bf16", tag=name + "_bf16", align_bytes=64)
-            dst = grouped[:].rearrange("p (c i) t -> p c t i", i=4)
-            src = raw[name][:].rearrange("p t (c i) -> p c t i", i=4)
-            if on_vector:
-                nc.vector.tensor_copy(out=dst, in_=src)
-            else:
-                nc.scalar.copy(out=dst, in_=src)
+        def cast(raw, name, shares):
+            grouped = keep.tile([P, raw.shape[2], PACK], BF16, name=name, tag=name, align_bytes=ALIGN)
+            for copy, cols in shares:
+                copy(
+                    out=grouped[:, cols, :].rearrange("p (c i) t -> p c t i", i=RUN),
+                    in_=raw[:, :, cols].rearrange("p t (c i) -> p c t i", i=RUN),
+                )
             return grouped
 
-        def quantize(grouped, name, cols=None, tag=None):
-            cols = cols or slice(0, grouped.shape[1])
-            width = cols.stop - cols.start
-            codes = keep.tile([P, width], U32, name=name + "_codes", tag=tag or name + "_codes", align_bytes=64)
-            scales = keep.tile([P, width], U8, name=name + "_scales", align_bytes=64)
-            nc.vector.quantize_mx(out=codes[:].bitcast(FP8X4), scales=scales[:], in_=grouped[:, cols, :].rearrange("p n t -> p (n t)"))
-            whole[name] = (codes, scales)
+        def quantize(grouped, name):
+            width = grouped.shape[1]
+            codes = keep.tile([P, width], U32, name=name + "_codes", align_bytes=ALIGN)
+            scales = keep.tile([P, width], U8, name=name + "_scales", align_bytes=ALIGN)
+            nc.vector.quantize_mx(
+                out=codes[:].bitcast(FP8X4), scales=scales[:], in_=grouped[:].rearrange("p n t -> p (n t)")
+            )
             return [(codes[:, c : c + M], scales[:, c : c + M]) for c in range(0, width, M)]
 
-        def load_list(d):
-            nc.sync.dma_start(lists[d][:], (offs, back1, back2)[d])
-
-        def load_scales(queue, rows):
-            for r in rows:
-                queue.dma_start(out=table_scales[r:P:32, :].bitcast(I32), in_=x_scales[0, r:16:4, :].bitcast(I32))
-
-        def load_words():
-            nc.sync.dma_start(out=table_words[:].bitcast(I32), in_=x_words[0].rearrange("p n t -> p (n t)").bitcast(I32))
-
         nc.vector.memset(table_scales[:].bitcast(I32), 0)
+
         warm_in = keep.tile([P, 1], F32, name="warm_in")
         warm_out = keep.tile([P, 1], F32, name="warm_out")
-        nc.vector.memset(warm_in[:], 0.0)
-        raw = {}
-        whole = {}
-        load_list(0)
-        load_list(1)
-        load_scales(nc.scalar, (2, 3))
-        load_scales(nc.sync, (0, 1))
+        nc.gpsimd.memset(warm_in[:], 0.0)
         nc.scalar.activation(out=warm_out[:], in_=warm_in[:], func=ACT.Sigmoid)
-        raw["v0"] = load(v0, "v0")
-        load_list(2)
-        load_words()
-        raw["v1"] = load(v1, "v1")
-        raw["v2"] = load(v2, "v2")
-        raw["w0"] = load(w0, "w0")
-        raw["w1"] = load(w1, "w1")
-        raw["w2a"] = load(w2, "w2a", slice(0, M))
-        raw["w2b"] = load(w2, "w2b", slice(M, N))
+
+        for tile, source in zip(lists, (offs, back1, back2)):
+            nc.sync.dma_start(tile[:], source)
+        for r in range(PACK):
+            nc.sync.dma_start(
+                out=table_scales[r:P:QUADRANT, :].bitcast(I32), in_=x_scales[0, r:SCALE_ROWS:PACK, :].bitcast(I32)
+            )
+        all_rows = slice(0, N)
+        v0_raw = load(v0, "v0_raw", all_rows)
+        nc.sync.dma_start(out=table_words[:].bitcast(I32), in_=x_words[0].rearrange("p n t -> p (n t)").bitcast(I32))
+        v1_raw = load(v1, "v1_raw", all_rows)
+        v2_raw = load(v2, "v2_raw", all_rows)
+        w0_raw = load(w0, "w0_raw", all_rows)
+        w1_raw = load(w1, "w1_raw", all_rows)
+        w2a_raw = load(w2, "w2a_raw", slice(0, M))
+        w2b_raw = load(w2, "w2b_raw", slice(M, N))
 
         picked_scales = []
-        for d in range(3):
-            ps = keep.tile([P, S], U8, name="picked_scales%d" % d, align_bytes=64)
-            nc.vector.tensor_copy(ps[:], table_scales[:].indirect(lists[d][:]))
-            picked_scales.append(ps)
+        for d in range(TAPS):
+            picked = keep.tile([P, S], U8, name="picked_scales%d" % d, align_bytes=ALIGN)
+            nc.vector.tensor_copy(picked[:], table_scales[:].indirect(lists[d][:]))
+            picked_scales.append(picked)
 
-        picked_words = {}
+        picked_words = []
 
         def gather_words(d, tag):
-            pw = keep.tile([P, S], U32, name="picked_words%d" % d, tag=tag, align_bytes=64)
-            nc.vector.tensor_copy(pw[:], table_words[:].indirect(lists[d][:]))
-            picked_words[d] = pw
+            picked = keep.tile([P, S], U32, name="picked_words%d" % d, tag=tag, align_bytes=ALIGN)
+            nc.vector.tensor_copy(picked[:], table_words[:].indirect(lists[d][:]))
+            picked_words.append(picked)
 
-        def product(bank, quantized, d, cols):
-            codes, scales = quantized
+        def product(bank, stationary, d, cols):
+            codes, scales = stationary
             nc.tensor.matmul_mx(
                 out=bank[:, 0 : cols.stop - cols.start],
                 lhsT=codes.bitcast(FP8X4),
@@ -110,66 +107,59 @@ def tile_picked_zwave_tanh_p_kernel(tc, x_words, x_scales, w0, v0, w1, v1, w2, v
                 rhs=picked_words[d][:, cols].bitcast(FP8X4),
                 rhs_scale=picked_scales[d][:, cols],
                 start=(d == 0),
-                stop=(d == 2),
+                stop=(d == TAPS - 1),
             )
 
-        pieces = [[(0, 256), (256, 512)], [(0, 256), (256, 384), (384, 512)]]
-        f_bank = {(m, c): psum.tile([P, 512], F32, name="f_bank%d_%d" % (m, c)) for m in range(2) for c, e in pieces[m]}
-        g_bank = [psum.tile([P, 512], F32, name="g_bank%d" % m) for m in range(2)]
+        row_tiles = range(N // M)
+        halves = [slice(c, c + HALF) for c in range(0, S, HALF)]
+        f_bank = [
+            [psum.tile([P, BANK], F32, name="f_bank%d_%d" % (m, cols.start)) for cols in halves] for m in row_tiles
+        ]
+        g_bank = [psum.tile([P, BANK], F32, name="g_bank%d" % m) for m in row_tiles]
 
         def g_products(quantized, d):
-            for m in range(2):
+            for m in row_tiles:
                 product(g_bank[m], quantized[m], d, slice(0, S))
 
-        def f_products(quantized, d, m):
-            for c, e in pieces[m]:
-                product(f_bank[m, c], quantized, d, slice(c, e))
+        def f_products(stationary, d, m):
+            for bank, cols in zip(f_bank[m], halves):
+                product(bank, stationary, d, cols)
 
-        def warm_tensor(name, passes):
-            codes, scales = whole[name]
-            spare = psum.tile([P, 512], F32, name="spare_bank")
-            for i in range(passes):
-                nc.tensor.matmul_mx(
-                    out=spare[:, 0:N],
-                    lhsT=codes[:, 0:M].bitcast(FP8X4),
-                    lhsT_scale=scales[:, 0:M],
-                    rhs=codes[:].bitcast(FP8X4),
-                    rhs_scale=scales[:],
-                    start=True,
-                    stop=True,
-                )
+        on_scalar = [(nc.scalar.copy, all_rows)]
 
-        def sigmoids(tag):
-            g = keep.tile([P, 2, S], F32, name="g", tag=tag, align_bytes=64)
-            for m in range(2):
-                nc.scalar.activation(out=g[:, m, :], in_=g_bank[m][:], func=ACT.Sigmoid)
-            return g
-
-        def finish(m):
-            for c, e in pieces[m]:
-                f = keep.tile([P, e - c], F32, name="f%d_%d" % (m, c))
-                nc.scalar.activation(out=f[:], in_=f_bank[m, c][:, 0 : e - c], func=ACT.Tanh)
-                y = keep.tile([P, e - c], F32, name="y%d_%d" % (m, c))
-                nc.vector.tensor_tensor(out=y[:], in0=f[:], in1=g[:, m, c:e], op=MULT)
-                nc.sync.dma_start(out=out[m * M : (m + 1) * M, c:e], in_=y[:])
-
-        qv0 = quantize(cast("v0"), "v0")
-        gather_words(0, "pw0")
-        g_products(qv0, 0)
-        gather_words(1, "pw1")
-        g_products(quantize(cast("v1"), "v1"), 1)
+        v0_q = quantize(cast(v0_raw, "v0_bf16", on_scalar), "v0")
+        gather_words(0, "picked_words0")
+        g_products(v0_q, 0)
+        gather_words(1, "picked_words1")
+        g_products(quantize(cast(v1_raw, "v1_bf16", on_scalar), "v1"), 1)
         gather_words(2, "v1_bf16")
-        g_products(quantize(cast("v2"), "v2"), 2)
-        qw0 = quantize(cast("w0"), "w0")
-        f_products(qw0[0], 0, 0)
-        f_products(qw0[1], 0, 1)
-        bw1 = cast("w1")
-        ba = cast("w2a", True)
-        qw1 = quantize(bw1, "w1")
-        f_products(qw1[0], 1, 0)
-        g = sigmoids("w1_raw")
-        f_products(quantize(ba, "w2a")[0], 2, 0)
-        f_products(qw1[1], 1, 1)
-        f_products(quantize(cast("w2b", True), "w2b")[0], 2, 1)
-        finish(0)
-        finish(1)
+        g_products(quantize(cast(v2_raw, "v2_bf16", on_scalar), "v2"), 2)
+
+        w0_q = quantize(cast(w0_raw, "w0_bf16", on_scalar), "w0")
+        for m in row_tiles:
+            f_products(w0_q[m], 0, m)
+        w1_bf16 = cast(w1_raw, "w1_bf16", on_scalar)
+        w2a_bf16 = cast(
+            w2a_raw,
+            "w2a_bf16",
+            [(nc.scalar.copy, slice(0, SCALAR_SHARE)), (nc.vector.tensor_copy, slice(SCALAR_SHARE, M))],
+        )
+        w2b_bf16 = cast(w2b_raw, "w2b_bf16", [(nc.vector.tensor_copy, slice(0, M))])
+        w1_q = quantize(w1_bf16, "w1")
+        f_products(w1_q[0], 1, 0)
+
+        gate = keep.tile([P, N // M, S], F32, name="gate", tag="w1_raw", align_bytes=ALIGN)
+        for m in row_tiles:
+            nc.scalar.activation(out=gate[:, m, :], in_=g_bank[m][:], func=ACT.Sigmoid)
+
+        f_products(quantize(w2a_bf16, "w2a")[0], 2, 0)
+        f_products(w1_q[1], 1, 1)
+        f_products(quantize(w2b_bf16, "w2b")[0], 2, 1)
+
+        for m in row_tiles:
+            for bank, cols in zip(f_bank[m], halves):
+                filtered = keep.tile([P, HALF], F32, name="filtered%d_%d" % (m, cols.start))
+                nc.scalar.activation(out=filtered[:], in_=bank[:, 0:HALF], func=ACT.Tanh)
+                result = keep.tile([P, HALF], F32, name="result%d_%d" % (m, cols.start))
+                nc.vector.tensor_tensor(out=result[:], in0=filtered[:], in1=gate[:, m, cols], op=MULT)
+                nc.sync.dma_start(out=out[m * M : (m + 1) * M, cols], in_=result[:])

from contextlib import ExitStack

import concourse.mybir as mybir

K, T, S, N = 512, 2048, 512, 256
TAPS = 3
FLOPS = 2 * (2 * TAPS) * K * N * S

F32 = mybir.dt.float32
BF16 = mybir.dt.bfloat16
I32 = mybir.dt.int32
U32 = mybir.dt.uint32
U16 = mybir.dt.uint16
U8 = mybir.dt.uint8
FP8X4 = mybir.dt.float8_e4m3fn_x4
ACT = mybir.ActivationFunctionType
MULT = mybir.AluOpType.mult

P = 128
PACK = 4
QUADRANT = 32
SCALE_ROWS = K // 32
LIST_GROUP = 16
RUN = 4
M = 128
BANK = 512
HALF = S // 2
ALIGN = 64
SCALAR_SHARE = 64


def tile_picked_zwave_tanh_p_kernel(tc, x_words, x_scales, w0, v0, w1, v1, w2, v2, offs, back1, back2, out):
    nc = tc.nc
    with ExitStack() as ctx:
        keep = ctx.enter_context(tc.tile_pool(name="keep", bufs=1))
        psum = ctx.enter_context(tc.psum_pool(name="psum", bufs=1))

        lists = [keep.tile([P, S // LIST_GROUP], U16, name="list%d" % d) for d in range(TAPS)]
        table_words = keep.tile([P, T], U32, name="table_words", align_bytes=ALIGN)
        table_scales = keep.tile([P, T], U8, name="table_scales", align_bytes=ALIGN)

        def load(weight, name, cols):
            raw = keep.tile([P, PACK, cols.stop - cols.start], F32, name=name, tag=name, align_bytes=ALIGN)
            nc.sync.dma_start(out=raw[:], in_=weight.rearrange("(p t) n -> p t n", t=PACK)[:, :, cols])
            return raw

        def cast(raw, name, shares):
            grouped = keep.tile([P, raw.shape[2], PACK], BF16, name=name, tag=name, align_bytes=ALIGN)
            for copy, cols in shares:
                copy(
                    out=grouped[:, cols, :].rearrange("p (c i) t -> p c t i", i=RUN),
                    in_=raw[:, :, cols].rearrange("p t (c i) -> p c t i", i=RUN),
                )
            return grouped

        def quantize(grouped, name):
            width = grouped.shape[1]
            codes = keep.tile([P, width], U32, name=name + "_codes", align_bytes=ALIGN)
            scales = keep.tile([P, width], U8, name=name + "_scales", align_bytes=ALIGN)
            nc.vector.quantize_mx(
                out=codes[:].bitcast(FP8X4), scales=scales[:], in_=grouped[:].rearrange("p n t -> p (n t)")
            )
            return [(codes[:, c : c + M], scales[:, c : c + M]) for c in range(0, width, M)]

        nc.vector.memset(table_scales[:].bitcast(I32), 0)

        warm_in = keep.tile([P, 1], F32, name="warm_in")
        warm_out = keep.tile([P, 1], F32, name="warm_out")
        nc.gpsimd.memset(warm_in[:], 0.0)
        nc.scalar.activation(out=warm_out[:], in_=warm_in[:], func=ACT.Sigmoid)

        for tile, source in zip(lists, (offs, back1, back2)):
            nc.sync.dma_start(tile[:], source)
        for r in range(PACK):
            nc.sync.dma_start(
                out=table_scales[r:P:QUADRANT, :].bitcast(I32), in_=x_scales[0, r:SCALE_ROWS:PACK, :].bitcast(I32)
            )
        all_rows = slice(0, N)
        v0_raw = load(v0, "v0_raw", all_rows)
        nc.sync.dma_start(out=table_words[:].bitcast(I32), in_=x_words[0].rearrange("p n t -> p (n t)").bitcast(I32))
        v1_raw = load(v1, "v1_raw", all_rows)
        v2_raw = load(v2, "v2_raw", all_rows)
        w0_raw = load(w0, "w0_raw", all_rows)
        w1_raw = load(w1, "w1_raw", all_rows)
        w2a_raw = load(w2, "w2a_raw", slice(0, M))
        w2b_raw = load(w2, "w2b_raw", slice(M, N))

        picked_scales = []
        for d in range(TAPS):
            picked = keep.tile([P, S], U8, name="picked_scales%d" % d, align_bytes=ALIGN)
            nc.vector.tensor_copy(picked[:], table_scales[:].indirect(lists[d][:]))
            picked_scales.append(picked)

        picked_words = []

        def gather_words(d, tag):
            picked = keep.tile([P, S], U32, name="picked_words%d" % d, tag=tag, align_bytes=ALIGN)
            nc.vector.tensor_copy(picked[:], table_words[:].indirect(lists[d][:]))
            picked_words.append(picked)

        def product(bank, stationary, d, cols):
            codes, scales = stationary
            nc.tensor.matmul_mx(
                out=bank[:, 0 : cols.stop - cols.start],
                lhsT=codes.bitcast(FP8X4),
                lhsT_scale=scales,
                rhs=picked_words[d][:, cols].bitcast(FP8X4),
                rhs_scale=picked_scales[d][:, cols],
                start=(d == 0),
                stop=(d == TAPS - 1),
            )

        row_tiles = range(N // M)
        halves = [slice(c, c + HALF) for c in range(0, S, HALF)]
        f_bank = [
            [psum.tile([P, BANK], F32, name="f_bank%d_%d" % (m, cols.start)) for cols in halves] for m in row_tiles
        ]
        g_bank = [psum.tile([P, BANK], F32, name="g_bank%d" % m) for m in row_tiles]

        def g_products(quantized, d):
            for m in row_tiles:
                product(g_bank[m], quantized[m], d, slice(0, S))

        def f_products(stationary, d, m):
            for bank, cols in zip(f_bank[m], halves):
                product(bank, stationary, d, cols)

        on_scalar = [(nc.scalar.copy, all_rows)]

        v0_q = quantize(cast(v0_raw, "v0_bf16", on_scalar), "v0")
        gather_words(0, "picked_words0")
        g_products(v0_q, 0)
        gather_words(1, "picked_words1")
        g_products(quantize(cast(v1_raw, "v1_bf16", on_scalar), "v1"), 1)
        gather_words(2, "v1_bf16")
        g_products(quantize(cast(v2_raw, "v2_bf16", on_scalar), "v2"), 2)

        w0_q = quantize(cast(w0_raw, "w0_bf16", on_scalar), "w0")
        for m in row_tiles:
            f_products(w0_q[m], 0, m)
        w1_bf16 = cast(w1_raw, "w1_bf16", on_scalar)
        w2a_bf16 = cast(
            w2a_raw,
            "w2a_bf16",
            [(nc.scalar.copy, slice(0, SCALAR_SHARE)), (nc.vector.tensor_copy, slice(SCALAR_SHARE, M))],
        )
        w2b_bf16 = cast(w2b_raw, "w2b_bf16", [(nc.vector.tensor_copy, slice(0, M))])
        w1_q = quantize(w1_bf16, "w1")
        f_products(w1_q[0], 1, 0)

        gate = keep.tile([P, N // M, S], F32, name="gate", tag="w1_raw", align_bytes=ALIGN)
        for m in row_tiles:
            nc.scalar.activation(out=gate[:, m, :], in_=g_bank[m][:], func=ACT.Sigmoid)

        f_products(quantize(w2a_bf16, "w2a")[0], 2, 0)
        f_products(w1_q[1], 1, 1)
        f_products(quantize(w2b_bf16, "w2b")[0], 2, 1)

        for m in row_tiles:
            for bank, cols in zip(f_bank[m], halves):
                filtered = keep.tile([P, HALF], F32, name="filtered%d_%d" % (m, cols.start))
                nc.scalar.activation(out=filtered[:], in_=bank[:, 0:HALF], func=ACT.Tanh)
                result = keep.tile([P, HALF], F32, name="result%d_%d" % (m, cols.start))
                nc.vector.tensor_tensor(out=result[:], in0=filtered[:], in1=gate[:, m, cols], op=MULT)
                nc.sync.dma_start(out=out[m * M : (m + 1) * M, cols], in_=result[:])
